import numpy as np
import ml_dtypes


def mxq(x, axis, fmt="e4m3"):
    dtype, down = {"e4m3": (ml_dtypes.float8_e4m3fn, 7), "e5m2": (ml_dtypes.float8_e5m2, 14)}[fmt]
    v = np.moveaxis(np.asarray(x, np.float32).astype(ml_dtypes.bfloat16).astype(np.float64), axis, -1)
    blocks = v.reshape(v.shape[:-1] + (-1, 32))
    amax = np.abs(blocks).max(-1, keepdims=True)
    byte = np.maximum(np.where(amax > 0, np.frexp(amax)[1] - 1 + 127, 0) - down, 1)
    scale = np.exp2(byte - 127.0)
    codes = (blocks / scale).astype(np.float32).astype(dtype).astype(np.float64)
    return np.moveaxis((codes * scale).reshape(v.shape), -1, axis)


WIDE = False


def mx_kscale(k):
    if not WIDE:
        return np.ones(k)
    levels = np.array([10, -10, 5, -5, 0])
    if k % 512:
        return np.exp2(np.random.permutation(np.resize(levels, k // 32))).repeat(32)
    a = np.empty((k // 512, 16))
    for p in range(k // 512):
        a[p, :8] = np.random.permutation(np.resize(levels, 8))
        for g in range(8):
            far = levels[np.abs(levels - a[p, g]) >= 10]
            a[p, g + 8] = far[np.random.randint(len(far))]
    return np.exp2(a.ravel()).repeat(32)


def f64(x):
    return np.asarray(x).astype(np.float64)


def striped(idx):
    return np.tile(np.asarray(idx).reshape(-1, 16).T, (8, 1)).astype(np.uint16)


def unstriped(offs):
    return offs[:16].T.reshape(-1).astype(np.int64)


E2M1 = np.array([0.0, 0.5, 1.0, 1.5, 2.0, 3.0, 4.0, 6.0, -0.0, -0.5, -1.0, -1.5, -2.0, -3.0, -4.0, -6.0])


def pack_weight(w, fmt):
    k, n = w.shape
    w = f64(np.asarray(w, np.float32).astype(ml_dtypes.bfloat16)).reshape(k // 32, 32, n)
    amax = np.abs(w).max(1)
    if fmt == "e4m3":
        byte = np.frexp(amax)[1] - 1 + 127 - 7
    else:
        mant, ex = np.frexp(amax / 6.0)
        byte = np.where(mant > 0.5, ex, ex - 1) + 127
    byte = np.clip(np.where(amax > 0, byte, 1), 1, 254)
    scaled = (w * np.exp2(127.0 - byte)[:, None, :]).reshape(k, n).astype(np.float32)
    by_word = np.ascontiguousarray(scaled.reshape(k // 512, 128, 4, n).transpose(0, 1, 3, 2))
    if fmt == "e4m3":
        words = by_word.astype(ml_dtypes.float8_e4m3fn).view(np.uint8)
    else:
        c = by_word.astype(ml_dtypes.float4_e2m1fn).view(np.uint8) & 0xF
        words = (c[..., 0::2] | (c[..., 1::2] << 4)).reshape(k // 512, 128, 2 * n)
    return np.ascontiguousarray(words), np.ascontiguousarray(byte.astype(np.uint8).reshape(k // 512, 16, n))


def unpack_weight(words, scales, fmt):
    g, _, n = scales.shape
    words = np.ascontiguousarray(words).reshape(g, 128, n, -1)
    if fmt == "e4m3":
        vals = words.view(ml_dtypes.float8_e4m3fn).astype(np.float64)
    else:
        nib = np.empty((g, 128, n, 4), np.uint8)
        nib[..., 0::2] = words & 0xF
        nib[..., 1::2] = words >> 4
        vals = E2M1[nib]
    vals = vals * np.repeat(np.exp2(scales.astype(np.float64) - 127.0), 8, axis=1)[..., None]
    return vals.transpose(0, 1, 3, 2).reshape(g * 512, n)


D, E, T, I, G, U, Q = 512, 512, 4096, 1024, 64, 512, 128


def setup_inputs():
    n = np.random.standard_normal
    idx = np.random.permutation(T)[:I]
    idx2 = np.random.permutation(U)[:G]
    fd = mx_kscale(D)
    fe = mx_kscale(E)
    keysp = pack_weight(n((D, T)) / fd[:, None], "e4m3")
    valsp = pack_weight(n((E, T)) / fe[:, None], "e4m3")
    return {
        "query": (n((D, Q)) * 0.8 / np.sqrt(D) * fd[:, None]).astype(np.float32),
        "keys_words": keysp[0],
        "keys_scales": keysp[1],
        "ptab": (0.5 * n((Q, U)) - 4.3).astype(np.float32),
        "gout": (n((E, Q)) * 1 / np.sqrt(E) * fe[:, None]).astype(np.float32),
        "vals_words": valsp[0],
        "vals_scales": valsp[1],
        "dquery": (n((D, Q)) * 1.0 / np.sqrt(D) * fd[:, None]).astype(np.float32),
        "base": (0.5 * n((Q, G))).astype(np.float32),
        "offs": striped(idx),
        "offs2": striped(idx2),
    }


def reference(query, keys_words, keys_scales, ptab, gout, vals_words, vals_scales, dquery, base, offs, offs2):
    idx = unstriped(offs)
    idx2 = unstriped(offs2)
    keysu = unpack_weight(keys_words, keys_scales, "e4m3")
    valsu = unpack_weight(vals_words, vals_scales, "e4m3")
    queryq = mxq(f64(query), 0, "e4m3")
    keysidxg = keysu[:, idx]
    a = queryq.T @ keysidxg
    dqueryq = mxq(f64(dquery), 0, "e4m3")
    ta = dqueryq.T @ keysidxg
    p = np.exp(a - np.max(a, axis=1, keepdims=True))
    z = np.sum(p, axis=1, keepdims=True)
    goutq = mxq(f64(gout), 0, "e4m3")
    valsidxg = valsu[:, idx]
    c0 = goutq.T @ valsidxg
    s = p.reshape(Q, G, I // G).sum(axis=2) / z
    m1 = (p * c0).reshape(Q, G, I // G).sum(axis=2) / z
    tp = np.exp(f64(ptab)[:, idx2])
    xp = ta * p
    xz = np.sum(xp, axis=1, keepdims=True)
    xs = (xp.reshape(Q, G, I // G).sum(axis=2) - xz * p.reshape(Q, G, I // G).sum(axis=2) / z) / z
    xm1 = ((xp * c0).reshape(Q, G, I // G).sum(axis=2) - xz * (p * c0).reshape(Q, G, I // G).sum(axis=2) / z) / z
    xdtp = ((xm1 - xs / tp * (1.0 + s / tp) * 2.0 * m1 / np.square(1.0 + s / tp)) / np.square(1.0 + s / tp) * (-1.0) * s + xs * m1 / np.square(1.0 + s / tp) * (-1.0)) / np.square(tp) * (-1.0)
    y = xdtp + f64(base)
    return y

@@ -1,0 +1,199 @@
+from contextlib import ExitStack
+
+import concourse.mybir as mybir
+from concourse.masks import make_identity
+
+F32 = mybir.dt.float32
+BF16 = mybir.dt.bfloat16
+I32 = mybir.dt.int32
+U32 = mybir.dt.uint32
+U16 = mybir.dt.uint16
+U8 = mybir.dt.uint8
+FP8X4 = mybir.dt.float8_e4m3fn_x4
+ALU = mybir.AluOpType
+ACT = mybir.ActivationFunctionType
+AX = mybir.AxisListType
+
+P = 128
+D = 512
+T = 4096
+SLOTS = 1024
+PAGES = 64
+PAGE = 16
+U = 512
+Q = 128
+HALF = 512
+HP = 32
+VALS_ROW = 4
+
+FLOPS = 3 * 2 * D * Q * SLOTS
+
+
+def tile_attend_hvpagecap_kernel(tc, query, keys_words, keys_scales, ptab, gout, vals_words, vals_scales, dquery, base, offs, offs2, out):
+    nc = tc.nc
+    with ExitStack() as ctx:
+        keep = ctx.enter_context(tc.tile_pool(name="keep", bufs=1))
+        psum = ctx.enter_context(tc.psum_pool(name="psum", bufs=1))
+
+        lst = keep.tile([P, SLOTS // 16], U16, name="lst")
+        nc.sync.dma_start(lst[:], offs)
+
+        def load_scales(src, name, row, zero_engine, queue):
+            win = keep.tile([P, T], U8, name=name, tag=name)
+            zero_engine.memset(win[:].bitcast(I32), 0)
+            for r in range(4):
+                queue.dma_start(win[row + r : P : 32, :].bitcast(I32), src[0, r:16:4, :].bitcast(I32))
+            return win
+
+        def load_words(src, name, tag):
+            win = keep.tile([P, T], U32, name=name, tag=tag)
+            nc.sync.dma_start(win[:].bitcast(I32), src[0].rearrange("p n t -> p (n t)").bitcast(I32))
+            return win
+
+        def load_rows(src, tag):
+            raw = keep.tile([P, 4, Q], F32, name="raw", tag=tag)
+            nc.sync.dma_start(raw[:], src.rearrange("(p j) w -> p j w", j=4))
+            return raw
+
+        def quantise(raw, name):
+            grouped = keep.tile([P, Q, 4], BF16, name=name + "_bf", align_bytes=64)
+            nc.scalar.copy(grouped[:], raw[:].rearrange("p j w -> p w j"))
+            codes = keep.tile([P, Q], U32, name=name + "_codes", align_bytes=64)
+            scales = keep.tile([P, Q], U8, name=name + "_scales", align_bytes=64)
+            nc.vector.quantize_mx(out=codes[:].bitcast(FP8X4), scales=scales[:], in_=grouped[:].rearrange("p w j -> p (w j)"))
+            return codes, scales
+
+        lst2 = keep.tile([P, PAGES // 16], U16, name="lst2")
+        nc.sync.dma_start(lst2[:], offs2)
+        q_raw = load_rows(query, "first")
+        dq_raw = load_rows(dquery, "second")
+        terms = keep.tile([P, 2, 5, HP], F32, name="terms")
+        nc.sync.dma_start(terms[:, :, 4, :], base.rearrange("q (h g) -> q h g", h=2))
+        ks_win = load_scales(keys_scales, "ks_win", 0, nc.vector, nc.sync)
+        one = keep.tile([P, 1], F32, name="one", tag="kw_win")
+        nc.vector.memset(one[:], 1.0)
+        consts = keep.tile([P, 2], F32, name="consts")
+        nc.vector.tensor_scalar_mul(consts[:, 0:1], one[:], -1.0)
+        nc.vector.tensor_scalar_mul(consts[:, 1:2], one[:], 0.5)
+        kw_win = load_words(keys_words, "kw_win", "kw_win")
+        vs_win = load_scales(vals_scales, "vs_win", VALS_ROW, nc.vector, nc.scalar)
+
+        warm = keep.tile([P, 1], F32, name="warm")
+        nc.scalar.activation(warm[:], consts[:, 0:1], ACT.Exp)
+
+        ident = keep.tile([P, P], F32, name="ident")
+        make_identity(nc, ident[:])
+
+        ks_g = keep.tile([P, SLOTS], U8, name="ks_g", align_bytes=64)
+        nc.vector.tensor_copy(ks_g[:], ks_win[:].indirect(lst[:]))
+        q_codes, q_scales = quantise(q_raw, "q")
+        vw_win = load_words(vals_words, "vw_win", "first")
+        vs_g = keep.tile([P, SLOTS], U8, name="vs_g", align_bytes=64)
+        nc.vector.tensor_copy(vs_g[:], vs_win[:].indirect(lst[:]))
+        dq_codes, dq_scales = quantise(dq_raw, "dq")
+        g_raw = load_rows(gout, "second")
+        pt_win = keep.tile([P, U], F32, name="pt_win", tag="ks_win")
+        nc.sync.dma_start(pt_win[:], ptab)
+
+        def gather_words(win, h, name):
+            g = keep.tile([P, HALF], U32, name=name + str(h), align_bytes=64)
+            nc.vector.tensor_copy(g[:], win[:].indirect(lst[:, h * 32 : (h + 1) * 32]))
+            return g
+
+        def product(codes, scales, words, plane, tag):
+            acc = psum.tile([P, HALF], F32, name=tag, tag=tag)
+            nc.tensor.matmul_mx(out=acc[:], lhsT=codes[:].bitcast(FP8X4), lhsT_scale=scales[:], rhs=words[:].bitcast(FP8X4), rhs_scale=plane, start=True, stop=True)
+            return acc
+
+        def by_place(acc):
+            return acc[:].rearrange("p (g j) -> p j g", j=PAGE)
+
+        a, ta = [], []
+        nmax2 = keep.tile([P, 2], F32, name="nmax2")
+        for h in range(2):
+            kg = gather_words(kw_win, h, "kg")
+            plane = ks_g[:, h * HALF : (h + 1) * HALF]
+            a.append(product(q_codes, q_scales, kg, plane, "a" + str(h)))
+            ta.append(product(dq_codes, dq_scales, kg, plane, "ta" + str(h)))
+        for h in range(2):
+            nc.vector.tensor_reduce(nmax2[:, h : h + 1], a[h][:], AX.X, ALU.max, negate=True)
+        nmax = keep.tile([P, 1], F32, name="nmax")
+        nc.vector.tensor_tensor(nmax[:], nmax2[:, 0:1], nmax2[:, 1:2], ALU.min)
+
+        x1 = keep.tile([P, PAGE, 2, PAGES], F32, name="x1")
+        for h in range(2):
+            hs = slice(h * HP, (h + 1) * HP)
+            nc.scalar.activation(x1[:, :, 0, hs], by_place(a[h]), ACT.Exp, bias=nmax[:])
+            nc.vector.tensor_tensor(x1[:, :, 1, hs], by_place(ta[h]), x1[:, :, 0, hs], ALU.mult)
+
+        def page_sums(src, n, tag_t, tag_b, name):
+            turned = psum.tile([P, P], F32, name=name + "_t", tag=tag_t)
+            for j in range(n):
+                nc.tensor.matmul(turned[:], lhsT=src[:, j * P : (j + 1) * P], rhs=ident[:], start=(j == 0), stop=(j == n - 1), is_transpose=True)
+            held = keep.tile([P, P], F32, name=name + "_held")
+            nc.scalar.copy(held[:], turned[:])
+            back = psum.tile([P, P], F32, name=name + "_b", tag=tag_b)
+            nc.tensor.transpose(back[:], held[:], ident[:])
+            return back
+
+        s1 = page_sums(x1[:].rearrange("p j k g -> p (j k g)"), PAGE, "s1t", "s1b", "s1")
+
+        g_codes, g_scales = quantise(g_raw, "g")
+        c0 = []
+        for h in range(2):
+            vg = gather_words(vw_win, h, "vg")
+            c0.append(product(g_codes, g_scales, vg, vs_g[VALS_ROW:P, h * HALF : (h + 1) * HALF], "c" + str(h)))
+
+        lt = keep.tile([P, PAGES], F32, name="lt")
+        nc.vector.tensor_copy(lt[:], pt_win[:].indirect(lst2[:]))
+        tp = keep.tile([P, PAGES], F32, name="tp")
+        nc.scalar.activation(tp[:], lt[:], ACT.Exp)
+
+        s2 = []
+        for h in range(2):
+            hs = slice(h * HP, (h + 1) * HP)
+            x2 = keep.tile([P, PAGE, 2, HP], F32, name="x2" + str(h))
+            for k in range(2):
+                nc.vector.tensor_tensor(x2[:, :, k, :], by_place(c0[h]), x1[:, :, k, hs], ALU.mult)
+            s2.append(page_sums(x2[:].rearrange("p j k g -> p (j k g)"), PAGE // 2, "a" + str(h), "ta" + str(h), "s2" + str(h)))
+
+        s1v = s1[:].rearrange("p (k g) -> p k g", k=2)
+        cz = keep.tile([P, PAGES + 2], F32, name="cz")
+        z = cz[:, PAGES : PAGES + 1]
+        xz = cz[:, PAGES + 1 : PAGES + 2]
+        nc.vector.tensor_reduce(cz[:, PAGES : PAGES + 2], s1v, AX.X, ALU.add)
+        nc.vector.scalar_tensor_tensor(cz[:, 0:PAGES], tp[:], z, s1v[:, 0, :], ALU.mult, ALU.add)
+        rec = keep.tile([P, PAGES + 1], F32, name="rec")
+        nc.vector.reciprocal(rec[:], cz[:, 0 : PAGES + 1])
+        rc = rec[:, 0:PAGES]
+        uw = keep.tile([P, 2, PAGES], F32, name="uw")
+        nc.vector.tensor_tensor(uw[:], s1v, rc.unsqueeze(1).to_broadcast([P, 2, PAGES]), ALU.mult)
+        u = uw[:, 0, :]
+        w = uw[:, 1, :]
+        mus = keep.tile([P, 2], F32, name="mus")
+        nc.vector.tensor_scalar(mus[:], consts[:], xz, rec[:, PAGES : PAGES + 1], ALU.mult, ALU.mult)
+        e = keep.tile([P, PAGES], F32, name="e")
+        nc.vector.scalar_tensor_tensor(e[:], u, mus[:, 0:1], w, ALU.mult, ALU.add)
+        coef = keep.tile([P, 2, PAGES], F32, name="coef")
+        nc.vector.tensor_tensor(coef[:, 1, :], u, rc, ALU.mult)
+        f = keep.tile([P, PAGES], F32, name="f")
+        nc.vector.scalar_tensor_tensor(f[:], u, -0.5, e[:], ALU.add, ALU.mult)
+        hh = keep.tile([P, PAGES], F32, name="hh")
+        nc.vector.scalar_tensor_tensor(hh[:], u, mus[:, 1:2], f[:], ALU.mult, ALU.add)
+        nc.vector.scalar_tensor_tensor(coef[:, 0, :], hh[:], -2.0, rc, ALU.mult, ALU.mult)
+
+        clk = keep.tile([P, 1], U8, name="clk")
+        nc.gpsimd.tensor_copy(clk[:], ks_g[:, 0:1])
+        clk2 = keep.tile([P, 1], F32, name="clk2")
+        nc.gpsimd.tensor_copy(clk2[:], x1[:, 0, 1, 63:64])
+        res = keep.tile([P, PAGES], F32, name="res")
+        for h in range(2):
+            hs = slice(h * HP, (h + 1) * HP)
+            nc.vector.tensor_tensor(
+                terms[:, h, 0:4, :].rearrange("p (i k) g -> p i k g", k=2),
+                s2[h][:].rearrange("p (i k g) -> p i k g", i=2, k=2),
+                coef[:, :, hs].unsqueeze(1).to_broadcast([P, 2, 2, HP]),
+                ALU.mult,
+            )
+            nc.vector.tensor_reduce(res[:, hs], terms[:, h, :, :].rearrange("p t g -> p g t"), AX.X, ALU.add)
+        nc.sync.dma_start(out, res[:])

@@ -33,67 +33,69 @@ def tile_attend_hvpagecap_kernel(tc, query, keys_words, keys_scales, ptab, gout,
     nc = tc.nc
     with ExitStack() as ctx:
         keep = ctx.enter_context(tc.tile_pool(name="keep", bufs=1))
+        shared = ctx.enter_context(tc.tile_pool(name="shared", bufs=1))
         psum = ctx.enter_context(tc.psum_pool(name="psum", bufs=1))
 
         lst = keep.tile([P, SLOTS // 16], U16, name="lst")
         nc.sync.dma_start(lst[:], offs)
 
-        def load_scales(src, name, row, zero_engine, queue):
-            win = keep.tile([P, T], U8, name=name, tag=name)
-            zero_engine.memset(win[:].bitcast(I32), 0)
-            for r in range(4):
-                queue.dma_start(win[row + r : P : 32, :].bitcast(I32), src[0, r:16:4, :].bitcast(I32))
+        def load_scales(src, win, row):
+            nc.sync.dma_start(win[row : row + 16, :].bitcast(I32), src[0].bitcast(I32))
+            nc.vector.memset(win[0:row, :].bitcast(I32), 0)
+            if row + 16 < P:
+                nc.vector.memset(win[row + 16 : P, :].bitcast(I32), 0)
             return win
 
-        def load_words(src, name, tag):
-            win = keep.tile([P, T], U32, name=name, tag=tag)
+        def gather_scales(win, row, name):
+            picked = keep.tile([P, SLOTS], U8, name=name + "_picked")
+            nc.vector.tensor_copy(picked[:], win[:].indirect(lst[:]))
+            plane = keep.tile([P, SLOTS], U8, name=name + "_plane", align_bytes=64)
+            nc.gpsimd.memset(plane[:].bitcast(I32), 0)
+            for r in range(4):
+                nc.scalar.dma_start(plane[r:P:32, :].bitcast(I32), picked[row + r : row + 16 : 4, :].bitcast(I32))
+            return plane
+
+        def load_words(src, win):
             nc.sync.dma_start(win[:].bitcast(I32), src[0].rearrange("p n t -> p (n t)").bitcast(I32))
             return win
 
-        def load_rows(src, tag):
-            raw = keep.tile([P, 4, Q], F32, name="raw", tag=tag)
+        def load_rows(src, raw):
             nc.sync.dma_start(raw[:], src.rearrange("(p j) w -> p j w", j=4))
             return raw
 
-        def quantise(raw, name):
-            grouped = keep.tile([P, Q, 4], BF16, name=name + "_bf", align_bytes=64)
-            nc.scalar.copy(grouped[:], raw[:].rearrange("p j w -> p w j"))
+        def quantise(raw, name, copy):
+            grouped = keep.tile([P, Q, 4], BF16, name=name + "_bf", tag=name + "_bf", align_bytes=64)
+            copy(grouped[:].rearrange("p (c i) j -> p c j i", i=4), raw[:].rearrange("p j (c i) -> p c j i", i=4))
             codes = keep.tile([P, Q], U32, name=name + "_codes", align_bytes=64)
             scales = keep.tile([P, Q], U8, name=name + "_scales", align_bytes=64)
             nc.vector.quantize_mx(out=codes[:].bitcast(FP8X4), scales=scales[:], in_=grouped[:].rearrange("p w j -> p (w j)"))
             return codes, scales
 
+        ks_win = load_scales(keys_scales, keep.tile([P, T], U8, name="ks_win"), 112)
+        vs_win = load_scales(vals_scales, shared.tile([P, T], U8, name="vs_win", offset=0), 48)
+        q_raw = load_rows(query, keep.tile([P, 4, Q], F32, name="q_raw"))
+        kw_win = load_words(keys_words, keep.tile([P, T], U32, name="kw_win"))
         lst2 = keep.tile([P, PAGES // 16], U16, name="lst2")
         nc.sync.dma_start(lst2[:], offs2)
-        q_raw = load_rows(query, "first")
-        dq_raw = load_rows(dquery, "second")
-        terms = keep.tile([P, 2, 5, HP], F32, name="terms")
-        nc.sync.dma_start(terms[:, :, 4, :], base.rearrange("q (h g) -> q h g", h=2))
-        ks_win = load_scales(keys_scales, "ks_win", 0, nc.vector, nc.sync)
-        one = keep.tile([P, 1], F32, name="one", tag="kw_win")
-        nc.vector.memset(one[:], 1.0)
+        dq_raw = load_rows(dquery, keep.tile([P, 4, Q], F32, name="dq_raw"))
+        g_raw = load_rows(gout, keep.tile([P, 4, Q], F32, name="g_raw"))
         consts = keep.tile([P, 2], F32, name="consts")
-        nc.vector.tensor_scalar_mul(consts[:, 0:1], one[:], -1.0)
-        nc.vector.tensor_scalar_mul(consts[:, 1:2], one[:], 0.5)
-        kw_win = load_words(keys_words, "kw_win", "kw_win")
-        vs_win = load_scales(vals_scales, "vs_win", VALS_ROW, nc.vector, nc.scalar)
-
+        nc.vector.memset(consts[:, 0:1], -1.0)
+        nc.vector.memset(consts[:, 1:2], 0.5)
         warm = keep.tile([P, 1], F32, name="warm")
         nc.scalar.activation(warm[:], consts[:, 0:1], ACT.Exp)
-
+        terms = keep.tile([P, 2, 5, HP], F32, name="terms")
+        nc.gpsimd.dma_start(terms[:, :, 4, :], base.rearrange("q (h g) -> q h g", h=2))
         ident = keep.tile([P, P], F32, name="ident")
         make_identity(nc, ident[:])
 
-        ks_g = keep.tile([P, SLOTS], U8, name="ks_g", align_bytes=64)
-        nc.vector.tensor_copy(ks_g[:], ks_win[:].indirect(lst[:]))
-        q_codes, q_scales = quantise(q_raw, "q")
-        vw_win = load_words(vals_words, "vw_win", "first")
-        vs_g = keep.tile([P, SLOTS], U8, name="vs_g", align_bytes=64)
-        nc.vector.tensor_copy(vs_g[:], vs_win[:].indirect(lst[:]))
-        dq_codes, dq_scales = quantise(dq_raw, "dq")
-        g_raw = load_rows(gout, "second")
-        pt_win = keep.tile([P, U], F32, name="pt_win", tag="ks_win")
+        ks_g = gather_scales(ks_win, 112, "ks")
+        q_codes, q_scales = quantise(q_raw, "q", nc.scalar.copy)
+        vs_g = gather_scales(vs_win, 48, "vs")
+        vw_win = load_words(vals_words, shared.tile([P, T], U32, name="vw_win", offset=2048))
+        pt_win = shared.tile([P, U], F32, name="pt_win", offset=0)
         nc.sync.dma_start(pt_win[:], ptab)
+        dq_codes, dq_scales = quantise(dq_raw, "dq", nc.scalar.copy)
 
         def gather_words(win, h, name):
             g = keep.tile([P, HALF], U32, name=name + str(h), align_bytes=64)
@@ -120,11 +122,14 @@ def tile_attend_hvpagecap_kernel(tc, query, keys_words, keys_scales, ptab, gout,
         nmax = keep.tile([P, 1], F32, name="nmax")
         nc.vector.tensor_tensor(nmax[:], nmax2[:, 0:1], nmax2[:, 1:2], ALU.min)
 
+        g_codes, g_scales = quantise(g_raw, "g", nc.scalar.copy)
+
         x1 = keep.tile([P, PAGE, 2, PAGES], F32, name="x1")
-        for h in range(2):
-            hs = slice(h * HP, (h + 1) * HP)
-            nc.scalar.activation(x1[:, :, 0, hs], by_place(a[h]), ACT.Exp, bias=nmax[:])
-            nc.vector.tensor_tensor(x1[:, :, 1, hs], by_place(ta[h]), x1[:, :, 0, hs], ALU.mult)
+        for js in (slice(0, 8), slice(8, 16)):
+            for h in range(2):
+                hs = slice(h * HP, (h + 1) * HP)
+                nc.scalar.activation(x1[:, js, 0, hs], by_place(a[h])[:, js, :], ACT.Exp, bias=nmax[:])
+                nc.vector.tensor_tensor(x1[:, js, 1, hs], by_place(ta[h])[:, js, :], x1[:, js, 0, hs], ALU.mult)
 
         def page_sums(src, n, tag_t, tag_b, name):
             turned = psum.tile([P, P], F32, name=name + "_t", tag=tag_t)
@@ -138,27 +143,18 @@ def tile_attend_hvpagecap_kernel(tc, query, keys_words, keys_scales, ptab, gout,
 
         s1 = page_sums(x1[:].rearrange("p j k g -> p (j k g)"), PAGE, "s1t", "s1b", "s1")
 
-        g_codes, g_scales = quantise(g_raw, "g")
         c0 = []
         for h in range(2):
             vg = gather_words(vw_win, h, "vg")
-            c0.append(product(g_codes, g_scales, vg, vs_g[VALS_ROW:P, h * HALF : (h + 1) * HALF], "c" + str(h)))
+            c0.append(product(g_codes, g_scales, vg, vs_g[:, h * HALF : (h + 1) * HALF], "c" + str(h)))
+
 
         lt = keep.tile([P, PAGES], F32, name="lt")
         nc.vector.tensor_copy(lt[:], pt_win[:].indirect(lst2[:]))
         tp = keep.tile([P, PAGES], F32, name="tp")
         nc.scalar.activation(tp[:], lt[:], ACT.Exp)
-
-        s2 = []
-        for h in range(2):
-            hs = slice(h * HP, (h + 1) * HP)
-            x2 = keep.tile([P, PAGE, 2, HP], F32, name="x2" + str(h))
-            for k in range(2):
-                nc.vector.tensor_tensor(x2[:, :, k, :], by_place(c0[h]), x1[:, :, k, hs], ALU.mult)
-            s2.append(page_sums(x2[:].rearrange("p j k g -> p (j k g)"), PAGE // 2, "a" + str(h), "ta" + str(h), "s2" + str(h)))
-
         s1v = s1[:].rearrange("p (k g) -> p k g", k=2)
-        cz = keep.tile([P, PAGES + 2], F32, name="cz")
+        cz = shared.tile([P, PAGES + 2], F32, name="cz", offset=2048)
         z = cz[:, PAGES : PAGES + 1]
         xz = cz[:, PAGES + 1 : PAGES + 2]
         nc.vector.tensor_reduce(cz[:, PAGES : PAGES + 2], s1v, AX.X, ALU.add)
@@ -182,10 +178,16 @@ def tile_attend_hvpagecap_kernel(tc, query, keys_words, keys_scales, ptab, gout,
         nc.vector.scalar_tensor_tensor(hh[:], u, mus[:, 1:2], f[:], ALU.mult, ALU.add)
         nc.vector.scalar_tensor_tensor(coef[:, 0, :], hh[:], -2.0, rc, ALU.mult, ALU.mult)
 
-        clk = keep.tile([P, 1], U8, name="clk")
-        nc.gpsimd.tensor_copy(clk[:], ks_g[:, 0:1])
-        clk2 = keep.tile([P, 1], F32, name="clk2")
-        nc.gpsimd.tensor_copy(clk2[:], x1[:, 0, 1, 63:64])
+        s2 = []
+        for h in range(2):
+            hs = slice(h * HP, (h + 1) * HP)
+            x2 = keep.tile([P, PAGE, 2, HP], F32, name="x2" + str(h))
+            step = 8 if h == 0 else 4
+            for j0 in range(0, PAGE, step):
+                js = slice(j0, j0 + step)
+                nc.vector.tensor_tensor(x2[:, js, :, :], by_place(c0[h])[:, js, :].unsqueeze(2).to_broadcast([P, step, 2, HP]), x1[:, js, :, hs], ALU.mult)
+            s2.append(page_sums(x2[:].rearrange("p j k g -> p (j k g)"), PAGE // 2, "a" + str(h), "ta" + str(h), "s2" + str(h)))
+
         res = keep.tile([P, PAGES], F32, name="res")
         for h in range(2):
             hs = slice(h * HP, (h + 1) * HP)

from contextlib import ExitStack

import concourse.mybir as mybir
from concourse.masks import make_identity

F32 = mybir.dt.float32
BF16 = mybir.dt.bfloat16
I32 = mybir.dt.int32
U32 = mybir.dt.uint32
U16 = mybir.dt.uint16
U8 = mybir.dt.uint8
FP8X4 = mybir.dt.float8_e4m3fn_x4
ALU = mybir.AluOpType
ACT = mybir.ActivationFunctionType
AX = mybir.AxisListType

P = 128
D = 512
T = 4096
SLOTS = 1024
PAGES = 64
PAGE = 16
U = 512
Q = 128
HALF = 512
HP = 32
VALS_ROW = 4

FLOPS = 3 * 2 * D * Q * SLOTS


def tile_attend_hvpagecap_kernel(tc, query, keys_words, keys_scales, ptab, gout, vals_words, vals_scales, dquery, base, offs, offs2, out):
    nc = tc.nc
    with ExitStack() as ctx:
        keep = ctx.enter_context(tc.tile_pool(name="keep", bufs=1))
        shared = ctx.enter_context(tc.tile_pool(name="shared", bufs=1))
        psum = ctx.enter_context(tc.psum_pool(name="psum", bufs=1))

        lst = keep.tile([P, SLOTS // 16], U16, name="lst")
        nc.sync.dma_start(lst[:], offs)

        def load_scales(src, win, row):
            nc.sync.dma_start(win[row : row + 16, :].bitcast(I32), src[0].bitcast(I32))
            nc.vector.memset(win[0:row, :].bitcast(I32), 0)
            if row + 16 < P:
                nc.vector.memset(win[row + 16 : P, :].bitcast(I32), 0)
            return win

        def gather_scales(win, row, name):
            picked = keep.tile([P, SLOTS], U8, name=name + "_picked")
            nc.vector.tensor_copy(picked[:], win[:].indirect(lst[:]))
            plane = keep.tile([P, SLOTS], U8, name=name + "_plane", align_bytes=64)
            nc.gpsimd.memset(plane[:].bitcast(I32), 0)
            for r in range(4):
                nc.scalar.dma_start(plane[r:P:32, :].bitcast(I32), picked[row + r : row + 16 : 4, :].bitcast(I32))
            return plane

        def load_words(src, win):
            nc.sync.dma_start(win[:].bitcast(I32), src[0].rearrange("p n t -> p (n t)").bitcast(I32))
            return win

        def load_rows(src, raw):
            nc.sync.dma_start(raw[:], src.rearrange("(p j) w -> p j w", j=4))
            return raw

        def quantise(raw, name, copy):
            grouped = keep.tile([P, Q, 4], BF16, name=name + "_bf", tag=name + "_bf", align_bytes=64)
            copy(grouped[:].rearrange("p (c i) j -> p c j i", i=4), raw[:].rearrange("p j (c i) -> p c j i", i=4))
            codes = keep.tile([P, Q], U32, name=name + "_codes", align_bytes=64)
            scales = keep.tile([P, Q], U8, name=name + "_scales", align_bytes=64)
            nc.vector.quantize_mx(out=codes[:].bitcast(FP8X4), scales=scales[:], in_=grouped[:].rearrange("p w j -> p (w j)"))
            return codes, scales

        ks_win = load_scales(keys_scales, keep.tile([P, T], U8, name="ks_win"), 112)
        vs_win = load_scales(vals_scales, shared.tile([P, T], U8, name="vs_win", offset=0), 48)
        q_raw = load_rows(query, keep.tile([P, 4, Q], F32, name="q_raw"))
        kw_win = load_words(keys_words, keep.tile([P, T], U32, name="kw_win"))
        lst2 = keep.tile([P, PAGES // 16], U16, name="lst2")
        nc.sync.dma_start(lst2[:], offs2)
        dq_raw = load_rows(dquery, keep.tile([P, 4, Q], F32, name="dq_raw"))
        g_raw = load_rows(gout, keep.tile([P, 4, Q], F32, name="g_raw"))
        consts = keep.tile([P, 2], F32, name="consts")
        nc.vector.memset(consts[:, 0:1], -1.0)
        nc.vector.memset(consts[:, 1:2], 0.5)
        warm = keep.tile([P, 1], F32, name="warm")
        nc.scalar.activation(warm[:], consts[:, 0:1], ACT.Exp)
        terms = keep.tile([P, 2, 5, HP], F32, name="terms")
        nc.gpsimd.dma_start(terms[:, :, 4, :], base.rearrange("q (h g) -> q h g", h=2))
        ident = keep.tile([P, P], F32, name="ident")
        make_identity(nc, ident[:])

        ks_g = gather_scales(ks_win, 112, "ks")
        q_codes, q_scales = quantise(q_raw, "q", nc.scalar.copy)
        vs_g = gather_scales(vs_win, 48, "vs")
        vw_win = load_words(vals_words, shared.tile([P, T], U32, name="vw_win", offset=2048))
        pt_win = shared.tile([P, U], F32, name="pt_win", offset=0)
        nc.sync.dma_start(pt_win[:], ptab)
        dq_codes, dq_scales = quantise(dq_raw, "dq", nc.scalar.copy)

        def gather_words(win, h, name):
            g = keep.tile([P, HALF], U32, name=name + str(h), align_bytes=64)
            nc.vector.tensor_copy(g[:], win[:].indirect(lst[:, h * 32 : (h + 1) * 32]))
            return g

        def product(codes, scales, words, plane, tag):
            acc = psum.tile([P, HALF], F32, name=tag, tag=tag)
            nc.tensor.matmul_mx(out=acc[:], lhsT=codes[:].bitcast(FP8X4), lhsT_scale=scales[:], rhs=words[:].bitcast(FP8X4), rhs_scale=plane, start=True, stop=True)
            return acc

        def by_place(acc):
            return acc[:].rearrange("p (g j) -> p j g", j=PAGE)

        a, ta = [], []
        nmax2 = keep.tile([P, 2], F32, name="nmax2")
        for h in range(2):
            kg = gather_words(kw_win, h, "kg")
            plane = ks_g[:, h * HALF : (h + 1) * HALF]
            a.append(product(q_codes, q_scales, kg, plane, "a" + str(h)))
            ta.append(product(dq_codes, dq_scales, kg, plane, "ta" + str(h)))
        for h in range(2):
            nc.vector.tensor_reduce(nmax2[:, h : h + 1], a[h][:], AX.X, ALU.max, negate=True)
        nmax = keep.tile([P, 1], F32, name="nmax")
        nc.vector.tensor_tensor(nmax[:], nmax2[:, 0:1], nmax2[:, 1:2], ALU.min)

        g_codes, g_scales = quantise(g_raw, "g", nc.scalar.copy)

        x1 = keep.tile([P, PAGE, 2, PAGES], F32, name="x1")
        for js in (slice(0, 8), slice(8, 16)):
            for h in range(2):
                hs = slice(h * HP, (h + 1) * HP)
                nc.scalar.activation(x1[:, js, 0, hs], by_place(a[h])[:, js, :], ACT.Exp, bias=nmax[:])
                nc.vector.tensor_tensor(x1[:, js, 1, hs], by_place(ta[h])[:, js, :], x1[:, js, 0, hs], ALU.mult)

        def page_sums(src, n, tag_t, tag_b, name):
            turned = psum.tile([P, P], F32, name=name + "_t", tag=tag_t)
            for j in range(n):
                nc.tensor.matmul(turned[:], lhsT=src[:, j * P : (j + 1) * P], rhs=ident[:], start=(j == 0), stop=(j == n - 1), is_transpose=True)
            held = keep.tile([P, P], F32, name=name + "_held")
            nc.scalar.copy(held[:], turned[:])
            back = psum.tile([P, P], F32, name=name + "_b", tag=tag_b)
            nc.tensor.transpose(back[:], held[:], ident[:])
            return back

        s1 = page_sums(x1[:].rearrange("p j k g -> p (j k g)"), PAGE, "s1t", "s1b", "s1")

        c0 = []
        for h in range(2):
            vg = gather_words(vw_win, h, "vg")
            c0.append(product(g_codes, g_scales, vg, vs_g[:, h * HALF : (h + 1) * HALF], "c" + str(h)))


        lt = keep.tile([P, PAGES], F32, name="lt")
        nc.vector.tensor_copy(lt[:], pt_win[:].indirect(lst2[:]))
        tp = keep.tile([P, PAGES], F32, name="tp")
        nc.scalar.activation(tp[:], lt[:], ACT.Exp)
        s1v = s1[:].rearrange("p (k g) -> p k g", k=2)
        cz = shared.tile([P, PAGES + 2], F32, name="cz", offset=2048)
        z = cz[:, PAGES : PAGES + 1]
        xz = cz[:, PAGES + 1 : PAGES + 2]
        nc.vector.tensor_reduce(cz[:, PAGES : PAGES + 2], s1v, AX.X, ALU.add)
        nc.vector.scalar_tensor_tensor(cz[:, 0:PAGES], tp[:], z, s1v[:, 0, :], ALU.mult, ALU.add)
        rec = keep.tile([P, PAGES + 1], F32, name="rec")
        nc.vector.reciprocal(rec[:], cz[:, 0 : PAGES + 1])
        rc = rec[:, 0:PAGES]
        uw = keep.tile([P, 2, PAGES], F32, name="uw")
        nc.vector.tensor_tensor(uw[:], s1v, rc.unsqueeze(1).to_broadcast([P, 2, PAGES]), ALU.mult)
        u = uw[:, 0, :]
        w = uw[:, 1, :]
        mus = keep.tile([P, 2], F32, name="mus")
        nc.vector.tensor_scalar(mus[:], consts[:], xz, rec[:, PAGES : PAGES + 1], ALU.mult, ALU.mult)
        e = keep.tile([P, PAGES], F32, name="e")
        nc.vector.scalar_tensor_tensor(e[:], u, mus[:, 0:1], w, ALU.mult, ALU.add)
        coef = keep.tile([P, 2, PAGES], F32, name="coef")
        nc.vector.tensor_tensor(coef[:, 1, :], u, rc, ALU.mult)
        f = keep.tile([P, PAGES], F32, name="f")
        nc.vector.scalar_tensor_tensor(f[:], u, -0.5, e[:], ALU.add, ALU.mult)
        hh = keep.tile([P, PAGES], F32, name="hh")
        nc.vector.scalar_tensor_tensor(hh[:], u, mus[:, 1:2], f[:], ALU.mult, ALU.add)
        nc.vector.scalar_tensor_tensor(coef[:, 0, :], hh[:], -2.0, rc, ALU.mult, ALU.mult)

        s2 = []
        for h in range(2):
            hs = slice(h * HP, (h + 1) * HP)
            x2 = keep.tile([P, PAGE, 2, HP], F32, name="x2" + str(h))
            step = 8 if h == 0 else 4
            for j0 in range(0, PAGE, step):
                js = slice(j0, j0 + step)
                nc.vector.tensor_tensor(x2[:, js, :, :], by_place(c0[h])[:, js, :].unsqueeze(2).to_broadcast([P, step, 2, HP]), x1[:, js, :, hs], ALU.mult)
            s2.append(page_sums(x2[:].rearrange("p j k g -> p (j k g)"), PAGE // 2, "a" + str(h), "ta" + str(h), "s2" + str(h)))

        res = keep.tile([P, PAGES], F32, name="res")
        for h in range(2):
            hs = slice(h * HP, (h + 1) * HP)
            nc.vector.tensor_tensor(
                terms[:, h, 0:4, :].rearrange("p (i k) g -> p i k g", k=2),
                s2[h][:].rearrange("p (i k g) -> p i k g", i=2, k=2),
                coef[:, :, hs].unsqueeze(1).to_broadcast([P, 2, 2, HP]),
                ALU.mult,
            )
            nc.vector.tensor_reduce(res[:, hs], terms[:, h, :, :].rearrange("p t g -> p g t"), AX.X, ALU.add)
        nc.sync.dma_start(out, res[:])
